import numpy as np
import ml_dtypes


def mxq(x, axis, fmt="e4m3"):
    dtype, down = {"e4m3": (ml_dtypes.float8_e4m3fn, 7), "e5m2": (ml_dtypes.float8_e5m2, 14)}[fmt]
    v = np.moveaxis(np.asarray(x, np.float32).astype(ml_dtypes.bfloat16).astype(np.float64), axis, -1)
    blocks = v.reshape(v.shape[:-1] + (-1, 32))
    amax = np.abs(blocks).max(-1, keepdims=True)
    byte = np.maximum(np.where(amax > 0, np.frexp(amax)[1] - 1 + 127, 0) - down, 1)
    scale = np.exp2(byte - 127.0)
    codes = (blocks / scale).astype(np.float32).astype(dtype).astype(np.float64)
    return np.moveaxis((codes * scale).reshape(v.shape), -1, axis)


WIDE = False


def mx_kscale(k):
    if not WIDE:
        return np.ones(k)
    levels = np.array([10, -10, 5, -5, 0])
    if k % 512:
        return np.exp2(np.random.permutation(np.resize(levels, k // 32))).repeat(32)
    a = np.empty((k // 512, 16))
    for p in range(k // 512):
        a[p, :8] = np.random.permutation(np.resize(levels, 8))
        for g in range(8):
            far = levels[np.abs(levels - a[p, g]) >= 10]
            a[p, g + 8] = far[np.random.randint(len(far))]
    return np.exp2(a.ravel()).repeat(32)


def f64(x):
    return np.asarray(x).astype(np.float64)


def striped8(idx):
    return np.concatenate([v.reshape(-1, 16).T for v in idx]).astype(np.uint16)


def unstriped8(offs):
    return np.stack([offs[16 * g:16 * g + 16].T.reshape(-1) for g in range(8)]).astype(np.int64)


E2M1 = np.array([0.0, 0.5, 1.0, 1.5, 2.0, 3.0, 4.0, 6.0, -0.0, -0.5, -1.0, -1.5, -2.0, -3.0, -4.0, -6.0])


def pack_weight(w, fmt):
    k, n = w.shape
    w = f64(np.asarray(w, np.float32).astype(ml_dtypes.bfloat16)).reshape(k // 32, 32, n)
    amax = np.abs(w).max(1)
    if fmt == "e4m3":
        byte = np.frexp(amax)[1] - 1 + 127 - 7
    else:
        mant, ex = np.frexp(amax / 6.0)
        byte = np.where(mant > 0.5, ex, ex - 1) + 127
    byte = np.clip(np.where(amax > 0, byte, 1), 1, 254)
    scaled = (w * np.exp2(127.0 - byte)[:, None, :]).reshape(k, n).astype(np.float32)
    by_word = np.ascontiguousarray(scaled.reshape(k // 512, 128, 4, n).transpose(0, 1, 3, 2))
    if fmt == "e4m3":
        words = by_word.astype(ml_dtypes.float8_e4m3fn).view(np.uint8)
    else:
        c = by_word.astype(ml_dtypes.float4_e2m1fn).view(np.uint8) & 0xF
        words = (c[..., 0::2] | (c[..., 1::2] << 4)).reshape(k // 512, 128, 2 * n)
    return np.ascontiguousarray(words), np.ascontiguousarray(byte.astype(np.uint8).reshape(k // 512, 16, n))


def unpack_weight(words, scales, fmt):
    g, _, n = scales.shape
    words = np.ascontiguousarray(words).reshape(g, 128, n, -1)
    if fmt == "e4m3":
        vals = words.view(ml_dtypes.float8_e4m3fn).astype(np.float64)
    else:
        nib = np.empty((g, 128, n, 4), np.uint8)
        nib[..., 0::2] = words & 0xF
        nib[..., 1::2] = words >> 4
        vals = E2M1[nib]
    vals = vals * np.repeat(np.exp2(scales.astype(np.float64) - 127.0), 8, axis=1)[..., None]
    return vals.transpose(0, 1, 3, 2).reshape(g * 512, n)


def gelu(v):
    return 0.5 * v * (1.0 + np.tanh(np.sqrt(2.0 / np.pi) * (v + 0.044715 * v**3)))


K, M, T, S = 1536, 1024, 1024, 512


def setup_inputs():
    n = np.random.standard_normal
    s = mx_kscale(K)[:, None]
    u = mx_kscale(512)[:, None]
    p_w4 = pack_weight(n((K, M)) / np.sqrt(K) / s, "e2m1")
    return {
        "x": (n((K, S)) * s).astype(np.float32),
        "w4_words": p_w4[0],
        "w4_scales": p_w4[1],
        "down": (n((K, 512)) / np.sqrt(K) / s * u.T).astype(np.float32),
        "up": (0.5 * n((512, M)) / np.sqrt(512) / u).astype(np.float32),
        "b": (0.3 * n(1024)).astype(np.float32),
        "wgo": np.repeat(np.random.uniform(0.5, 2.0, (8, S)), 16, axis=0).astype(np.float32),
        "offs": striped8(np.stack([np.random.permutation(T)[:S] for _ in range(8)])),
    }


def reference(x, w4_words, w4_scales, down, up, b, wgo, offs):
    x_ = mxq(f64(x), 0, "e4m3")
    w4_ = unpack_weight(w4_words, w4_scales, "e2m1")
    down_ = mxq(f64(down), 0, "e4m3")
    up_ = mxq(f64(up), 0, "e4m3")
    h_ = mxq(down_.T @ x_, 0, "e4m3")
    y = w4_.T @ x_ + up_.T @ h_
    place = unstriped8(offs)[np.arange(M) % 128 // 16]
    out = np.zeros((M, T))
    out[np.arange(M)[:, None], place] = f64(wgo)[np.arange(M) % 128] * (gelu(y + f64(b)[:, None]))
    return out

from contextlib import ExitStack

import concourse.mybir as mybir
from concourse.masks import make_identity

K, M, T, S, R = 1536, 1024, 1024, 512, 512
FLOPS = 2 * S * (K * R + K * M + R * M)

F32 = mybir.dt.float32
BF16 = mybir.dt.bfloat16
I32 = mybir.dt.int32
U32 = mybir.dt.uint32
U16 = mybir.dt.uint16
U8 = mybir.dt.uint8
FP8X4 = mybir.dt.float8_e4m3fn_x4
FP4X4 = mybir.dt.float4_e2m1fn_x4
GELU = mybir.ActivationFunctionType.Gelu_apprx_tanh
MULT = mybir.AluOpType.mult

P = 128
PACK = 4
K_PASS = P * PACK
PASSES = K // K_PASS
TILES = M // P
HALF = S // 2
CHUNK = 128
CHUNKS = HALF // CHUNK
BANK = 512
W_GROUP = 4
QUADRANTS = 4


def tile_list_hscat_l_gelu_kernel(tc, x, w4_words, w4_scales, down, up, b, wgo, offs, out):
    nc = tc.nc
    with ExitStack() as ctx:
        keep = ctx.enter_context(tc.tile_pool(name="keep", bufs=1))
        psum = ctx.enter_context(tc.psum_pool(name="psum", bufs=1))

        def mx_tiles(name, width):
            codes = keep.tile([P, width], U32, name=name + "_codes", align_bytes=64)
            scales = keep.tile([P, width], U8, name=name + "_scales", align_bytes=64)
            return codes, scales

        def quantize(operand, c0, c1, rounded):
            codes, scales = operand
            nc.vector.quantize_mx(out=codes[:, c0:c1].bitcast(FP8X4), scales=scales[:, c0:c1],
                                  in_=rounded[:, PACK * c0:PACK * c1])

        def copy_on(engine, dst, src):
            if engine == "vector":
                nc.vector.tensor_copy(out=dst, in_=src)
            else:
                nc.scalar.copy(out=dst, in_=src)

        def bank(i, name):
            return psum.tile([P, BANK], F32, name=name, tag="bank%d" % i)

        def load_rows(name, rows):
            raw = keep.tile([P, PACK, rows.shape[1]], F32, name=name, tag=name)
            nc.sync.dma_start(out=raw[:], in_=rows.rearrange("(p j) w -> p j w", j=PACK))
            return raw

        def load_down(a):
            return load_rows("down_raw%d" % a, down[a * K_PASS:(a + 1) * K_PASS, :])

        def load_x(half, a):
            return load_rows("x_raw%d_%d" % (half, a), x[a * K_PASS:(a + 1) * K_PASS, half * HALF:(half + 1) * HALF])

        def load_up(pair):
            return load_rows("up_raw%d" % pair, up[:, 2 * pair * P:2 * (pair + 1) * P])

        def load_w4_scales(group, plane):
            cols = slice(group * W_GROUP * P, (group + 1) * W_GROUP * P)
            for q in range(QUADRANTS):
                nc.sync.dma_start(
                    out=plane[32 * q:32 * q + 4, :, :].bitcast(I32),
                    in_=w4_scales[:, 4 * q:4 * q + 4, cols].rearrange("a r n -> r a n").bitcast(I32))

        def load_w4_words(group):
            width = 2 * W_GROUP * P
            words = keep.tile([P, PASSES, width], U8, name="w4_words%d" % group, align_bytes=64)
            nc.sync.dma_start(
                out=words[:].bitcast(I32),
                in_=w4_words[:, :, group * width:(group + 1) * width].rearrange("a p n -> p a n").bitcast(I32))
            return words

        def load_wgo(half):
            weights = keep.tile([P, HALF], F32, name="wgo%d" % half)
            nc.sync.dma_start(out=weights[:], in_=wgo[:, half * HALF:(half + 1) * HALF])
            return weights

        offsets = keep.tile([P, S // 16], U16, name="offsets")

        w4_planes = []
        for group in range(TILES // W_GROUP):
            plane = keep.tile([P, PASSES, W_GROUP * P], U8, name="w4_plane%d" % group, align_bytes=64)
            nc.vector.memset(plane[:].bitcast(U32), 0)
            w4_planes.append(plane)

        b_rows = keep.tile([P, P], F32, name="b_rows")
        ident = keep.tile([P, P], F32, name="ident")
        nc.vector.memset(b_rows[:], 0.0)
        make_identity(nc, ident[:])
        warm = keep.tile([P, 1], F32, name="warm")
        nc.scalar.activation(out=warm[:], in_=b_rows[:, 0:1], func=GELU)

        down_raw, x_raw, up_raw, w4_tiles, wgo_tiles = {}, {}, {}, {}, {}
        down_raw[0] = load_down(0)
        x_raw[0, 0] = load_x(0, 0)
        down_raw[1] = load_down(1)
        down_raw[2] = load_down(2)
        x_raw[0, 1] = load_x(0, 1)
        x_raw[0, 2] = load_x(0, 2)
        nc.sync.dma_start(out=b_rows[0:TILES, :], in_=b.rearrange("(c p) -> c p", p=P))
        load_w4_scales(0, w4_planes[0])
        up_raw[0] = load_up(0)
        w4_tiles[0] = load_w4_words(0)
        nc.sync.dma_start(offsets[:], offs)
        wgo_tiles[0] = load_wgo(0)
        up_raw[1] = load_up(1)
        load_w4_scales(1, w4_planes[1])
        w4_tiles[1] = load_w4_words(1)
        up_raw[2] = load_up(2)
        for a in range(PASSES):
            x_raw[1, a] = load_x(1, a)
        up_raw[3] = load_up(3)
        wgo_tiles[1] = load_wgo(1)

        b_cols = keep.tile([P, TILES], F32, name="b_cols")

        def interleave(engine, rounded, raw, dst0, src0, width):
            copy_on(engine,
                    rounded[:, PACK * dst0:PACK * (dst0 + width)].rearrange("p (c i t) -> p c t i", i=4, t=PACK),
                    raw[:, :, src0:src0 + width].rearrange("p t (c i) -> p c t i", i=4))

        down_mx, x_mx, up_mx, h_mx, h_banks = {}, {}, {}, {}, {}

        def prepare_down(a):
            rounded = keep.tile([P, PACK * R], BF16, name="down_bf%d" % a, align_bytes=64)
            nc.vector.tensor_copy(out=rounded[:].rearrange("p (t m j) -> p m j t", t=PACK, j=PACK),
                                  in_=down_raw[a][:].rearrange("p j (m t) -> p m j t", t=PACK))
            down_mx[a] = mx_tiles("down%d" % a, R)
            quantize(down_mx[a], 0, R, rounded)

        def prepare_x(half, a, engines):
            rounded = keep.tile([P, PACK * HALF], BF16, name="x_bf%d_%d" % (half, a), align_bytes=64)
            x_mx[half, a] = mx_tiles("x%d_%d" % (half, a), HALF)
            width = HALF // len(engines)
            for i, engine in enumerate(engines):
                interleave(engine, rounded, x_raw[half, a], i * width, i * width, width)
            for i in range(len(engines)):
                quantize(x_mx[half, a], i * width, (i + 1) * width, rounded)

        def prepare_up(c):
            rounded = keep.tile([P, PACK * P], BF16, name="up_bf%d" % c, align_bytes=64)
            up_mx[c] = mx_tiles("up%d" % c, P)
            interleave("scalar", rounded, up_raw[c // 2], 0, (c % 2) * P, P)
            quantize(up_mx[c], 0, P, rounded)

        def h_pass(half, a):
            for chunk in range(CHUNKS):
                if a == 0:
                    h_banks[half, chunk] = bank(chunk, "h_bank%d_%d" % (half, chunk))
                cols = slice(chunk * CHUNK, (chunk + 1) * CHUNK)
                for t in range(PACK):
                    rows = slice(t * P, (t + 1) * P)
                    nc.tensor.matmul_mx(
                        out=h_banks[half, chunk][:, t * CHUNK:(t + 1) * CHUNK],
                        lhsT=down_mx[a][0][:, rows].bitcast(FP8X4), lhsT_scale=down_mx[a][1][:, rows],
                        rhs=x_mx[half, a][0][:, cols].bitcast(FP8X4), rhs_scale=x_mx[half, a][1][:, cols],
                        start=(a == 0 and t == 0), stop=(a == PASSES - 1 and t == PACK - 1))

        def finish_h(half, engines):
            rounded = keep.tile([P, PACK * HALF], BF16, name="h_bf%d" % half, align_bytes=64)
            h_mx[half] = mx_tiles("h%d" % half, HALF)
            for chunk in range(CHUNKS):
                copy_on(engines[chunk],
                        rounded[:, PACK * chunk * CHUNK:PACK * (chunk + 1) * CHUNK].rearrange("p (n t) -> p n t", t=PACK),
                        h_banks[half, chunk][:].rearrange("p (t n) -> p n t", t=PACK))
            for chunk in range(CHUNKS):
                quantize(h_mx[half], chunk * CHUNK, (chunk + 1) * CHUNK, rounded)

        windows = {}

        def clear_window(c):
            windows[c] = keep.tile([P, T], F32, name="window%d" % c)
            nc.vector.memset(windows[c][:].bitcast(I32), 0)

        def unit(half, c, bank_index, tag):
            acc = bank(bank_index, "y%d_%d" % (half, c))
            words, plane = w4_tiles[c // W_GROUP], w4_planes[c // W_GROUP]
            n0 = (c % W_GROUP) * P
            for a in range(PASSES):
                for chunk in range(CHUNKS):
                    cols = slice(chunk * CHUNK, (chunk + 1) * CHUNK)
                    nc.tensor.matmul_mx(
                        out=acc[:, cols],
                        lhsT=words[:, a, 2 * n0:2 * (n0 + P)].bitcast(FP4X4), lhsT_scale=plane[:, a, n0:n0 + P],
                        rhs=x_mx[half, a][0][:, cols].bitcast(FP8X4), rhs_scale=x_mx[half, a][1][:, cols],
                        start=(a == 0 and chunk == 0), stop=False)
            nc.tensor.matmul_mx(
                out=acc[:, 0:HALF],
                lhsT=up_mx[c][0][:].bitcast(FP8X4), lhsT_scale=up_mx[c][1][:],
                rhs=h_mx[half][0][:].bitcast(FP8X4), rhs_scale=h_mx[half][1][:],
                start=False, stop=True)
            values = keep.tile([P, HALF], F32, name="values%d_%d" % (half, c), tag=tag)
            nc.scalar.activation(out=values[:], in_=acc[:, 0:HALF], func=GELU, bias=b_cols[:, c:c + 1])
            list_cols = slice(half * HALF // 16, (half + 1) * HALF // 16)
            nc.vector.tensor_tensor(windows[c][:].indirect(offsets[:, list_cols]), values[:], wgo_tiles[half][:], MULT)
            if half == 1:
                nc.sync.dma_start(out=out[c * P:(c + 1) * P, :], in_=windows[c][:])

        prepare_down(0)
        prepare_x(0, 0, ["scalar"])
        h_pass(0, 0)
        prepare_down(1)
        prepare_down(2)
        prepare_x(0, 1, ["scalar"])
        h_pass(0, 1)
        prepare_x(0, 2, ["vector", "scalar"])
        h_pass(0, 2)
        b_bank = bank(7, "b_bank")
        nc.tensor.transpose(b_bank[:, 0:P], b_rows[:], ident[:])
        nc.scalar.copy(out=b_cols[:], in_=b_bank[:, 0:TILES])
        prepare_up(0)
        finish_h(0, ["vector", "scalar"])
        for c in range(TILES):
            clear_window(c)

        unit(0, 0, 2, "values0_0")
        prepare_up(1)
        prepare_up(2)
        prepare_up(3)
        unit(0, 1, 3, "up_raw1")
        prepare_up(4)
        prepare_up(5)
        unit(0, 2, 4, "up_raw2")
        prepare_x(1, 0, ["scalar"])
        h_pass(1, 0)
        prepare_x(1, 1, ["scalar"])
        h_pass(1, 1)
        unit(0, 3, 5, "x_raw1_1")
        prepare_x(1, 2, ["scalar"])
        h_pass(1, 2)
        unit(0, 4, 6, "x_raw1_2")
        prepare_up(6)
        prepare_up(7)
        unit(0, 5, 7, "up_raw3")
        finish_h(1, ["scalar", "scalar"])
        unit(0, 6, 2, "values0_6")
        unit(0, 7, 1, "values0_7")
        for c in range(TILES):
            unit(1, c, 2 + (c + 1) % 6, "values1_%d" % c)
